import numpy as np
import ml_dtypes


def mxq(x, axis, fmt="e4m3"):
    dtype, down = {"e4m3": (ml_dtypes.float8_e4m3fn, 7), "e5m2": (ml_dtypes.float8_e5m2, 14)}[fmt]
    v = np.moveaxis(np.asarray(x, np.float32).astype(ml_dtypes.bfloat16).astype(np.float64), axis, -1)
    blocks = v.reshape(v.shape[:-1] + (-1, 32))
    amax = np.abs(blocks).max(-1, keepdims=True)
    byte = np.maximum(np.where(amax > 0, np.frexp(amax)[1] - 1 + 127, 0) - down, 1)
    scale = np.exp2(byte - 127.0)
    codes = (blocks / scale).astype(np.float32).astype(dtype).astype(np.float64)
    return np.moveaxis((codes * scale).reshape(v.shape), -1, axis)


WIDE = False


def mx_kscale(k):
    if not WIDE:
        return np.ones(k)
    levels = np.array([10, -10, 5, -5, 0])
    if k % 512:
        return np.exp2(np.random.permutation(np.resize(levels, k // 32))).repeat(32)
    a = np.empty((k // 512, 16))
    for p in range(k // 512):
        a[p, :8] = np.random.permutation(np.resize(levels, 8))
        for g in range(8):
            far = levels[np.abs(levels - a[p, g]) >= 10]
            a[p, g + 8] = far[np.random.randint(len(far))]
    return np.exp2(a.ravel()).repeat(32)


def f64(x):
    return np.asarray(x).astype(np.float64)


def striped(idx):
    return np.tile(idx.reshape(-1, 16).T, (8, 1)).astype(np.uint16)


def unstriped(offs):
    return offs[:16].T.reshape(-1).astype(np.int64)


K, T, D, S, V, N = 1024, 2048, 8, 4096, 512, 128


def setup_inputs():
    n = np.random.standard_normal
    s = mx_kscale(K)[:, None]
    return {
        "xT": (n((K, T)) * s).astype(np.float32),
        "w": (n((K, N)) / np.sqrt(K) / s).astype(np.float32),
        "b": (0.3 * n((N, 1))).astype(np.float32),
        "offs": striped(np.concatenate([np.random.permutation(T)[:V] for _ in range(D)])),
    }


def reference(xT, w, b, offs):
    idx = unstriped(offs)
    x = np.empty((K, V))
    for l in range(D):
        r = l // 4 * (4 * K // D) + l % 4 + 4 * np.arange(K // D)
        x[r] = f64(xT)[r][:, idx[l * V:(l + 1) * V]]
    xq = mxq(x, 0, "e4m3")
    return (mxq(f64(w), 0, "e4m3").T @ xq) + f64(b)

@@ -1,0 +1,107 @@
+from contextlib import ExitStack
+
+import concourse.mybir as mybir
+
+K, T, LEVELS, V, N = 1024, 2048, 8, 512, 128
+FLOPS = 2 * K * N * V
+
+F32 = mybir.dt.float32
+BF16 = mybir.dt.bfloat16
+U32 = mybir.dt.uint32
+U16 = mybir.dt.uint16
+U8 = mybir.dt.uint8
+FP8X4 = mybir.dt.float8_e4m3fn_x4
+ADD = mybir.AluOpType.add
+IDENTITY = mybir.ActivationFunctionType.Identity
+
+P = 128
+PACK = 4
+PASSES = K // (P * PACK)
+HALF = V // 2
+CHUNKS = ((0, 256), (256, 384), (384, 512))
+COLS = V // 16
+
+
+def tile_picked_grid_lin_bias_sub_l_kernel(tc, xT, w, b, offs, out):
+    nc = tc.nc
+    x_rows = xT.rearrange("(g p t) c -> g t p c", p=P, t=PACK)
+    w_rows = w.rearrange("(g p t) m -> g p t m", p=P, t=PACK)
+
+    with ExitStack() as ctx:
+        keep = ctx.enter_context(tc.tile_pool(name="keep", bufs=1))
+        psum = ctx.enter_context(tc.psum_pool(name="psum", bufs=1))
+
+        offsets = keep.tile([P, LEVELS * COLS], U16, name="offsets")
+        bias = keep.tile([P, 1], F32, name="bias")
+        tables = [keep.tile([P, T], F32, name=f"table{l}") for l in range(LEVELS)]
+        w_raw = [keep.tile([P, PACK, N], F32, name=f"w_raw{g}") for g in range(PASSES)]
+        w_grouped = [keep.tile([P, N, PACK], BF16, name=f"w_grouped{g}", align_bytes=64) for g in range(PASSES)]
+        w_codes = [keep.tile([P, N], U32, name=f"w_codes{g}", align_bytes=64) for g in range(PASSES)]
+        w_scales = [keep.tile([P, N], U8, name=f"w_scales{g}", align_bytes=64) for g in range(PASSES)]
+        grouped = [keep.tile([P, V, PACK], BF16, name=f"grouped{g}", align_bytes=64) for g in range(PASSES)]
+        codes = [keep.tile([P, V], U32, name=f"codes{g}", align_bytes=64) for g in range(PASSES)]
+        scales = [keep.tile([P, V], U8, name=f"scales{g}", align_bytes=64) for g in range(PASSES)]
+        acc = [psum.tile([N, v1 - v0], F32, name=f"acc{v0}") for v0, v1 in CHUNKS]
+        result = [keep.tile([N, v1 - v0], F32, name=f"result{v0}") for v0, v1 in CHUNKS]
+
+        nc.sync.dma_start(offsets[:], offs)
+        for l in range(LEVELS):
+            nc.sync.dma_start(tables[l][:], x_rows[l // PACK, l % PACK])
+        for g in range(PASSES):
+            nc.sync.dma_start(w_raw[g][:], w_rows[g])
+        nc.sync.dma_start(bias[:], b)
+
+        def gather(l, v0, v1):
+            picked = offsets[:, l * COLS + v0 // 16 : l * COLS + v1 // 16]
+            nc.vector.tensor_copy(grouped[l // PACK][:, v0:v1, l % PACK], tables[l][:].indirect(picked))
+
+        def quantize(g, v0, v1):
+            nc.vector.quantize_mx(
+                out=codes[g][:, v0:v1].bitcast(FP8X4),
+                scales=scales[g][:, v0:v1],
+                in_=grouped[g][:, v0:v1, :].rearrange("p v t -> p (v t)"),
+            )
+
+        def quantize_w(g):
+            nc.vector.quantize_mx(
+                out=w_codes[g][:].bitcast(FP8X4),
+                scales=w_scales[g][:],
+                in_=w_grouped[g][:].rearrange("p m t -> p (m t)"),
+            )
+
+        def multiply(g, h):
+            v0, v1 = CHUNKS[h]
+            nc.tensor.matmul_mx(
+                out=acc[h][:],
+                lhsT=w_codes[g][:].bitcast(FP8X4),
+                lhsT_scale=w_scales[g][:],
+                rhs=codes[g][:, v0:v1].bitcast(FP8X4),
+                rhs_scale=scales[g][:, v0:v1],
+                start=(g == 0),
+                stop=(g == PASSES - 1),
+            )
+
+        for l in range(PACK):
+            gather(l, 0, V)
+        gather(4, 0, V)
+        quantize(0, 0, V)
+        gather(5, 0, V)
+        gather(6, 0, V)
+        gather(7, 0, HALF)
+        gather(7, HALF, V)
+        for g in range(PASSES):
+            nc.scalar.copy(w_grouped[g][:], w_raw[g][:].rearrange("p t m -> p m t"))
+        quantize_w(0)
+        quantize(1, *CHUNKS[0])
+        quantize_w(1)
+        quantize(1, *CHUNKS[1])
+        quantize(1, *CHUNKS[2])
+        for g in range(PASSES):
+            for h in range(len(CHUNKS)):
+                multiply(g, h)
+        for h, (v0, v1) in enumerate(CHUNKS):
+            if h == len(CHUNKS) - 1:
+                nc.vector.tensor_scalar(result[h][:], acc[h][:], bias[:], None, ADD)
+            else:
+                nc.scalar.activation(result[h][:], acc[h][:], IDENTITY, bias=bias[:])
+            nc.sync.dma_start(out[:, v0:v1], result[h][:])

@@ -31,10 +31,10 @@ def tile_picked_grid_lin_bias_sub_l_kernel(tc, xT, w, b, offs, out):
         keep = ctx.enter_context(tc.tile_pool(name="keep", bufs=1))
         psum = ctx.enter_context(tc.psum_pool(name="psum", bufs=1))
 
-        offsets = keep.tile([P, LEVELS * COLS], U16, name="offsets")
+        offsets = keep.tile([P, LEVELS * COLS], U16, name="offsets", align_bytes=256)
         bias = keep.tile([P, 1], F32, name="bias")
-        tables = [keep.tile([P, T], F32, name=f"table{l}") for l in range(LEVELS)]
-        w_raw = [keep.tile([P, PACK, N], F32, name=f"w_raw{g}") for g in range(PASSES)]
+        tables = [keep.tile([P, T], F32, name=f"table{l}", align_bytes=256) for l in range(LEVELS)]
+        w_raw = [keep.tile([P, PACK, N], F32, name=f"w_raw{g}", align_bytes=256) for g in range(PASSES)]
         w_grouped = [keep.tile([P, N, PACK], BF16, name=f"w_grouped{g}", align_bytes=64) for g in range(PASSES)]
         w_codes = [keep.tile([P, N], U32, name=f"w_codes{g}", align_bytes=64) for g in range(PASSES)]
         w_scales = [keep.tile([P, N], U8, name=f"w_scales{g}", align_bytes=64) for g in range(PASSES)]
@@ -42,7 +42,7 @@ def tile_picked_grid_lin_bias_sub_l_kernel(tc, xT, w, b, offs, out):
         codes = [keep.tile([P, V], U32, name=f"codes{g}", align_bytes=64) for g in range(PASSES)]
         scales = [keep.tile([P, V], U8, name=f"scales{g}", align_bytes=64) for g in range(PASSES)]
         acc = [psum.tile([N, v1 - v0], F32, name=f"acc{v0}") for v0, v1 in CHUNKS]
-        result = [keep.tile([N, v1 - v0], F32, name=f"result{v0}") for v0, v1 in CHUNKS]
+        result = [keep.tile([N, v1 - v0], F32, name=f"result{v0}", align_bytes=256) for v0, v1 in CHUNKS]
 
         nc.sync.dma_start(offsets[:], offs)
         for l in range(LEVELS):

@@ -34,12 +34,20 @@ def tile_picked_grid_lin_bias_sub_l_kernel(tc, xT, w, b, offs, out):
         offsets = keep.tile([P, LEVELS * COLS], U16, name="offsets", align_bytes=256)
         bias = keep.tile([P, 1], F32, name="bias")
         tables = [keep.tile([P, T], F32, name=f"table{l}", align_bytes=256) for l in range(LEVELS)]
-        w_raw = [keep.tile([P, PACK, N], F32, name=f"w_raw{g}", align_bytes=256) for g in range(PASSES)]
+        w_raw = [keep.tile([P, PACK, N], F32, name=f"w_raw{g}", tag=f"shared{g}", align_bytes=256) for g in range(PASSES)]
         w_grouped = [keep.tile([P, N, PACK], BF16, name=f"w_grouped{g}", align_bytes=64) for g in range(PASSES)]
         w_codes = [keep.tile([P, N], U32, name=f"w_codes{g}", align_bytes=64) for g in range(PASSES)]
         w_scales = [keep.tile([P, N], U8, name=f"w_scales{g}", align_bytes=64) for g in range(PASSES)]
         grouped = [keep.tile([P, V, PACK], BF16, name=f"grouped{g}", align_bytes=64) for g in range(PASSES)]
-        codes = [keep.tile([P, V], U32, name=f"codes{g}", align_bytes=64) for g in range(PASSES)]
+        codes0 = keep.tile([P, V], U32, name="codes0", align_bytes=64)
+        late_codes = []
+
+        def codes(g, v0, v1):
+            if g == 0:
+                return codes0[:, v0:v1].bitcast(FP8X4)
+            half = v0 // HALF
+            return late_codes[half][:, v0 - half * HALF : v1 - half * HALF].bitcast(FP8X4)
+
         scales = [keep.tile([P, V], U8, name=f"scales{g}", align_bytes=64) for g in range(PASSES)]
         acc = [psum.tile([N, v1 - v0], F32, name=f"acc{v0}") for v0, v1 in CHUNKS]
         result = [keep.tile([N, v1 - v0], F32, name=f"result{v0}", align_bytes=256) for v0, v1 in CHUNKS]
@@ -57,7 +65,7 @@ def tile_picked_grid_lin_bias_sub_l_kernel(tc, xT, w, b, offs, out):
 
         def quantize(g, v0, v1):
             nc.vector.quantize_mx(
-                out=codes[g][:, v0:v1].bitcast(FP8X4),
+                out=codes(g, v0, v1),
                 scales=scales[g][:, v0:v1],
                 in_=grouped[g][:, v0:v1, :].rearrange("p v t -> p (v t)"),
             )
@@ -75,7 +83,7 @@ def tile_picked_grid_lin_bias_sub_l_kernel(tc, xT, w, b, offs, out):
                 out=acc[h][:],
                 lhsT=w_codes[g][:].bitcast(FP8X4),
                 lhsT_scale=w_scales[g][:],
-                rhs=codes[g][:, v0:v1].bitcast(FP8X4),
+                rhs=codes(g, v0, v1),
                 rhs_scale=scales[g][:, v0:v1],
                 start=(g == 0),
                 stop=(g == PASSES - 1),
@@ -91,6 +99,7 @@ def tile_picked_grid_lin_bias_sub_l_kernel(tc, xT, w, b, offs, out):
         gather(7, HALF, V)
         for g in range(PASSES):
             nc.scalar.copy(w_grouped[g][:], w_raw[g][:].rearrange("p t m -> p m t"))
+            late_codes.append(keep.tile([P, HALF], U32, name=f"codes1_{g}", tag=f"shared{g}", align_bytes=256))
         quantize_w(0)
         quantize(1, *CHUNKS[0])
         quantize_w(1)

@@ -18,7 +18,8 @@ P = 128
 PACK = 4
 PASSES = K // (P * PACK)
 HALF = V // 2
-CHUNKS = ((0, 256), (256, 384), (384, 512))
+CHUNK = 128
+CHUNKS = tuple((v0, v0 + CHUNK) for v0 in range(0, V, CHUNK))
 COLS = V // 16
 
 
@@ -50,7 +51,7 @@ def tile_picked_grid_lin_bias_sub_l_kernel(tc, xT, w, b, offs, out):
 
         scales = [keep.tile([P, V], U8, name=f"scales{g}", align_bytes=64) for g in range(PASSES)]
         acc = [psum.tile([N, v1 - v0], F32, name=f"acc{v0}") for v0, v1 in CHUNKS]
-        result = [keep.tile([N, v1 - v0], F32, name=f"result{v0}", align_bytes=256) for v0, v1 in CHUNKS]
+        result = [keep.tile([N, HALF], F32, name=f"result{half}", align_bytes=256) for half in range(2)]
 
         nc.sync.dma_start(offsets[:], offs)
         for l in range(LEVELS):
@@ -98,19 +99,21 @@ def tile_picked_grid_lin_bias_sub_l_kernel(tc, xT, w, b, offs, out):
         gather(7, 0, HALF)
         gather(7, HALF, V)
         for g in range(PASSES):
-            nc.scalar.copy(w_grouped[g][:], w_raw[g][:].rearrange("p t m -> p m t"))
+            nc.scalar.copy(
+                w_grouped[g][:].rearrange("p (c i) t -> p c t i", i=PACK),
+                w_raw[g][:].rearrange("p t (c i) -> p c t i", i=PACK),
+            )
             late_codes.append(keep.tile([P, HALF], U32, name=f"codes1_{g}", tag=f"shared{g}", align_bytes=256))
         quantize_w(0)
         quantize(1, *CHUNKS[0])
-        quantize_w(1)
         quantize(1, *CHUNKS[1])
+        quantize_w(1)
         quantize(1, *CHUNKS[2])
+        quantize(1, *CHUNKS[3])
         for g in range(PASSES):
             for h in range(len(CHUNKS)):
                 multiply(g, h)
-        for h, (v0, v1) in enumerate(CHUNKS):
-            if h == len(CHUNKS) - 1:
-                nc.vector.tensor_scalar(result[h][:], acc[h][:], bias[:], None, ADD)
-            else:
-                nc.scalar.activation(result[h][:], acc[h][:], IDENTITY, bias=bias[:])
-            nc.sync.dma_start(out[:, v0:v1], result[h][:])
+        for half in range(2):
+            nc.scalar.activation(result[half][:, :CHUNK], acc[2 * half][:], IDENTITY, bias=bias[:])
+            nc.vector.tensor_scalar(result[half][:, CHUNK:], acc[2 * half + 1][:], bias[:], None, ADD)
+            nc.sync.dma_start(out[:, half * HALF : (half + 1) * HALF], result[half][:])

@@ -19,7 +19,7 @@ PACK = 4
 PASSES = K // (P * PACK)
 HALF = V // 2
 CHUNK = 128
-CHUNKS = tuple((v0, v0 + CHUNK) for v0 in range(0, V, CHUNK))
+CHUNKS = V // CHUNK
 COLS = V // 16
 
 
@@ -38,20 +38,13 @@ def tile_picked_grid_lin_bias_sub_l_kernel(tc, xT, w, b, offs, out):
         w_raw = [keep.tile([P, PACK, N], F32, name=f"w_raw{g}", tag=f"shared{g}", align_bytes=256) for g in range(PASSES)]
         w_grouped = [keep.tile([P, N, PACK], BF16, name=f"w_grouped{g}", align_bytes=64) for g in range(PASSES)]
         w_codes = [keep.tile([P, N], U32, name=f"w_codes{g}", align_bytes=64) for g in range(PASSES)]
-        w_scales = [keep.tile([P, N], U8, name=f"w_scales{g}", align_bytes=64) for g in range(PASSES)]
         grouped = [keep.tile([P, V, PACK], BF16, name=f"grouped{g}", align_bytes=64) for g in range(PASSES)]
         codes0 = keep.tile([P, V], U32, name="codes0", align_bytes=64)
-        late_codes = []
-
-        def codes(g, v0, v1):
-            if g == 0:
-                return codes0[:, v0:v1].bitcast(FP8X4)
-            half = v0 // HALF
-            return late_codes[half][:, v0 - half * HALF : v1 - half * HALF].bitcast(FP8X4)
-
         scales = [keep.tile([P, V], U8, name=f"scales{g}", align_bytes=64) for g in range(PASSES)]
-        acc = [psum.tile([N, v1 - v0], F32, name=f"acc{v0}") for v0, v1 in CHUNKS]
-        result = [keep.tile([N, HALF], F32, name=f"result{half}", align_bytes=256) for half in range(2)]
+        w_scales0 = keep.tile([P, N], U8, name="w_scales0", align_bytes=64)
+        w_scales = [w_scales0[:], scales[0][4:, V - N :]]
+        acc = [psum.tile([N, CHUNK], F32, name=f"acc{h}") for h in range(CHUNKS)]
+        result = [keep.tile([N, CHUNK], F32, name=f"result{h}", align_bytes=256) for h in range(CHUNKS)]
 
         nc.sync.dma_start(offsets[:], offs)
         for l in range(LEVELS):
@@ -64,36 +57,13 @@ def tile_picked_grid_lin_bias_sub_l_kernel(tc, xT, w, b, offs, out):
             picked = offsets[:, l * COLS + v0 // 16 : l * COLS + v1 // 16]
             nc.vector.tensor_copy(grouped[l // PACK][:, v0:v1, l % PACK], tables[l][:].indirect(picked))
 
-        def quantize(g, v0, v1):
-            nc.vector.quantize_mx(
-                out=codes(g, v0, v1),
-                scales=scales[g][:, v0:v1],
-                in_=grouped[g][:, v0:v1, :].rearrange("p v t -> p (v t)"),
-            )
-
-        def quantize_w(g):
-            nc.vector.quantize_mx(
-                out=w_codes[g][:].bitcast(FP8X4),
-                scales=w_scales[g][:],
-                in_=w_grouped[g][:].rearrange("p m t -> p (m t)"),
-            )
-
-        def multiply(g, h):
-            v0, v1 = CHUNKS[h]
-            nc.tensor.matmul_mx(
-                out=acc[h][:],
-                lhsT=w_codes[g][:].bitcast(FP8X4),
-                lhsT_scale=w_scales[g][:],
-                rhs=codes(g, v0, v1),
-                rhs_scale=scales[g][:, v0:v1],
-                start=(g == 0),
-                stop=(g == PASSES - 1),
-            )
+        def quantize(codes, scale_bytes, values):
+            nc.vector.quantize_mx(out=codes.bitcast(FP8X4), scales=scale_bytes, in_=values.rearrange("p c t -> p (c t)"))
 
         for l in range(PACK):
             gather(l, 0, V)
         gather(4, 0, V)
-        quantize(0, 0, V)
+        quantize(codes0[:], scales[0][:], grouped[0][:])
         gather(5, 0, V)
         gather(6, 0, V)
         gather(7, 0, HALF)
@@ -103,17 +73,38 @@ def tile_picked_grid_lin_bias_sub_l_kernel(tc, xT, w, b, offs, out):
                 w_grouped[g][:].rearrange("p (c i) t -> p c t i", i=PACK),
                 w_raw[g][:].rearrange("p t (c i) -> p c t i", i=PACK),
             )
-            late_codes.append(keep.tile([P, HALF], U32, name=f"codes1_{g}", tag=f"shared{g}", align_bytes=256))
-        quantize_w(0)
-        quantize(1, *CHUNKS[0])
-        quantize(1, *CHUNKS[1])
-        quantize_w(1)
-        quantize(1, *CHUNKS[2])
-        quantize(1, *CHUNKS[3])
-        for g in range(PASSES):
-            for h in range(len(CHUNKS)):
-                multiply(g, h)
-        for half in range(2):
-            nc.scalar.activation(result[half][:, :CHUNK], acc[2 * half][:], IDENTITY, bias=bias[:])
-            nc.vector.tensor_scalar(result[half][:, CHUNK:], acc[2 * half + 1][:], bias[:], None, ADD)
-            nc.sync.dma_start(out[:, half * HALF : (half + 1) * HALF], result[half][:])
+        codes1_first = keep.tile([P, CHUNK], U32, name="codes1_first", tag="shared0", align_bytes=256)
+        codes1_rest = keep.tile([P, V - CHUNK], U32, name="codes1_rest", tag="shared1", align_bytes=256)
+        codes = [
+            [codes0[:, h * CHUNK : (h + 1) * CHUNK] for h in range(CHUNKS)],
+            [codes1_first[:]] + [codes1_rest[:, h * CHUNK : (h + 1) * CHUNK] for h in range(CHUNKS - 1)],
+        ]
+
+        def quantize_chunk(h):
+            points = slice(h * CHUNK, (h + 1) * CHUNK)
+            quantize(codes[1][h], scales[1][:, points], grouped[1][:, points, :])
+
+        def multiply(g, h):
+            nc.tensor.matmul_mx(
+                out=acc[h][:],
+                lhsT=w_codes[g][:].bitcast(FP8X4),
+                lhsT_scale=w_scales[g],
+                rhs=codes[g][h].bitcast(FP8X4),
+                rhs_scale=scales[g][:, h * CHUNK : (h + 1) * CHUNK],
+                start=(g == 0),
+                stop=(g == PASSES - 1),
+            )
+
+        quantize(w_codes[0][:], w_scales[0], w_grouped[0][:])
+        quantize_chunk(0)
+        quantize(w_codes[1][:], w_scales[1], w_grouped[1][:])
+        for h in range(1, CHUNKS):
+            quantize_chunk(h)
+        for g, h in ((0, 0), (0, 1), (0, 2), (1, 0), (1, 1), (1, 2), (0, 3), (1, 3)):
+            multiply(g, h)
+        for h in range(CHUNKS):
+            if h % 2 == 0:
+                nc.scalar.activation(result[h][:], acc[h][:], IDENTITY, bias=bias[:])
+            else:
+                nc.vector.tensor_scalar(result[h][:], acc[h][:], bias[:], None, ADD)
+            nc.sync.dma_start(out[:, h * CHUNK : (h + 1) * CHUNK], result[h][:])

@@ -46,8 +46,9 @@ def tile_picked_grid_lin_bias_sub_l_kernel(tc, xT, w, b, offs, out):
         acc = [psum.tile([N, CHUNK], F32, name=f"acc{h}") for h in range(CHUNKS)]
         result = [keep.tile([N, CHUNK], F32, name=f"result{h}", align_bytes=256) for h in range(CHUNKS)]
 
+        nc.sync.dma_start(tables[0][:], x_rows[0, 0])
         nc.sync.dma_start(offsets[:], offs)
-        for l in range(LEVELS):
+        for l in range(1, LEVELS):
             nc.sync.dma_start(tables[l][:], x_rows[l // PACK, l % PACK])
         for g in range(PASSES):
             nc.sync.dma_start(w_raw[g][:], w_rows[g])

@@ -20,6 +20,7 @@ PASSES = K // (P * PACK)
 HALF = V // 2
 CHUNK = 128
 CHUNKS = V // CHUNK
+PLAIN = 96
 COLS = V // 16
 
 
@@ -30,12 +31,13 @@ def tile_picked_grid_lin_bias_sub_l_kernel(tc, xT, w, b, offs, out):
 
     with ExitStack() as ctx:
         keep = ctx.enter_context(tc.tile_pool(name="keep", bufs=1))
+        tail = ctx.enter_context(tc.tile_pool(name="tail", bufs=1))
         psum = ctx.enter_context(tc.psum_pool(name="psum", bufs=1))
 
         offsets = keep.tile([P, LEVELS * COLS], U16, name="offsets", align_bytes=256)
         bias = keep.tile([P, 1], F32, name="bias")
         tables = [keep.tile([P, T], F32, name=f"table{l}", align_bytes=256) for l in range(LEVELS)]
-        w_raw = [keep.tile([P, PACK, N], F32, name=f"w_raw{g}", tag=f"shared{g}", align_bytes=256) for g in range(PASSES)]
+        w_raw = [tail.tile([P, PACK, N], F32, name=f"w_raw{g}", align_bytes=256, offset=2048 * g) for g in range(PASSES)]
         w_grouped = [keep.tile([P, N, PACK], BF16, name=f"w_grouped{g}", align_bytes=64) for g in range(PASSES)]
         w_codes = [keep.tile([P, N], U32, name=f"w_codes{g}", align_bytes=64) for g in range(PASSES)]
         grouped = [keep.tile([P, V, PACK], BF16, name=f"grouped{g}", align_bytes=64) for g in range(PASSES)]
@@ -67,15 +69,15 @@ def tile_picked_grid_lin_bias_sub_l_kernel(tc, xT, w, b, offs, out):
         quantize(codes0[:], scales[0][:], grouped[0][:])
         gather(5, 0, V)
         gather(6, 0, V)
-        gather(7, 0, HALF)
-        gather(7, HALF, V)
+        gather(7, 0, V - PLAIN)
         for g in range(PASSES):
             nc.scalar.copy(
                 w_grouped[g][:].rearrange("p (c i) t -> p c t i", i=PACK),
                 w_raw[g][:].rearrange("p t (c i) -> p c t i", i=PACK),
             )
-        codes1_first = keep.tile([P, CHUNK], U32, name="codes1_first", tag="shared0", align_bytes=256)
-        codes1_rest = keep.tile([P, V - CHUNK], U32, name="codes1_rest", tag="shared1", align_bytes=256)
+        last_plain = tail.tile([P, PLAIN], BF16, name="last_plain", align_bytes=256, offset=1024)
+        codes1_first = tail.tile([P, CHUNK], U32, name="codes1_first", align_bytes=256, offset=0)
+        codes1_rest = tail.tile([P, V - CHUNK], U32, name="codes1_rest", align_bytes=256, offset=2048)
         codes = [
             [codes0[:, h * CHUNK : (h + 1) * CHUNK] for h in range(CHUNKS)],
             [codes1_first[:]] + [codes1_rest[:, h * CHUNK : (h + 1) * CHUNK] for h in range(CHUNKS - 1)],
@@ -97,6 +99,8 @@ def tile_picked_grid_lin_bias_sub_l_kernel(tc, xT, w, b, offs, out):
             )
 
         quantize(w_codes[0][:], w_scales[0], w_grouped[0][:])
+        nc.vector.tensor_copy(last_plain[:], tables[7][:].indirect(offsets[:, LEVELS * COLS - PLAIN // 16 :]))
+        nc.scalar.copy(grouped[1][:, V - PLAIN :, PACK - 1], last_plain[:])
         quantize_chunk(0)
         quantize(w_codes[1][:], w_scales[1], w_grouped[1][:])
         for h in range(1, CHUNKS):

@@ -17,11 +17,11 @@ IDENTITY = mybir.ActivationFunctionType.Identity
 P = 128
 PACK = 4
 PASSES = K // (P * PACK)
-HALF = V // 2
 CHUNK = 128
 CHUNKS = V // CHUNK
-PLAIN = 96
 COLS = V // 16
+HALF = V // 2
+SHARE = N // 2
 
 
 def tile_picked_grid_lin_bias_sub_l_kernel(tc, xT, w, b, offs, out):
@@ -37,14 +37,16 @@ def tile_picked_grid_lin_bias_sub_l_kernel(tc, xT, w, b, offs, out):
         offsets = keep.tile([P, LEVELS * COLS], U16, name="offsets", align_bytes=256)
         bias = keep.tile([P, 1], F32, name="bias")
         tables = [keep.tile([P, T], F32, name=f"table{l}", align_bytes=256) for l in range(LEVELS)]
-        w_raw = [tail.tile([P, PACK, N], F32, name=f"w_raw{g}", align_bytes=256, offset=2048 * g) for g in range(PASSES)]
-        w_grouped = [keep.tile([P, N, PACK], BF16, name=f"w_grouped{g}", align_bytes=64) for g in range(PASSES)]
+        w_raw = [tail.tile([P, PACK, N], F32, name=f"w_raw{g}", align_bytes=256, offset=3072 * g) for g in range(PASSES)]
+        w_grouped0 = keep.tile([P, N, PACK], BF16, name="w_grouped0", align_bytes=64)
+        w_grouped1_scalar = keep.tile([P, N - SHARE, PACK], BF16, name="w_grouped1_scalar", align_bytes=64)
         w_codes = [keep.tile([P, N], U32, name=f"w_codes{g}", align_bytes=64) for g in range(PASSES)]
-        grouped = [keep.tile([P, V, PACK], BF16, name=f"grouped{g}", align_bytes=64) for g in range(PASSES)]
+        w_scales = [keep.tile([P, N], U8, name=f"w_scales{g}", align_bytes=64) for g in range(PASSES)]
+        grouped0 = keep.tile([P, V, PACK], BF16, name="grouped0", align_bytes=64)
+        grouped1 = keep.tile([P, HALF, PACK], BF16, name="grouped1", align_bytes=64)
+        pairs = keep.tile([P, 2, HALF], U32, name="pairs", align_bytes=64)
         codes0 = keep.tile([P, V], U32, name="codes0", align_bytes=64)
         scales = [keep.tile([P, V], U8, name=f"scales{g}", align_bytes=64) for g in range(PASSES)]
-        w_scales0 = keep.tile([P, N], U8, name="w_scales0", align_bytes=64)
-        w_scales = [w_scales0[:], scales[0][4:, V - N :]]
         acc = [psum.tile([N, CHUNK], F32, name=f"acc{h}") for h in range(CHUNKS)]
         result = [keep.tile([N, CHUNK], F32, name=f"result{h}", align_bytes=256) for h in range(CHUNKS)]
 
@@ -56,57 +58,70 @@ def tile_picked_grid_lin_bias_sub_l_kernel(tc, xT, w, b, offs, out):
             nc.sync.dma_start(w_raw[g][:], w_rows[g])
         nc.sync.dma_start(bias[:], b)
 
-        def gather(l, v0, v1):
+        def gather(values, l, v0, v1):
             picked = offsets[:, l * COLS + v0 // 16 : l * COLS + v1 // 16]
-            nc.vector.tensor_copy(grouped[l // PACK][:, v0:v1, l % PACK], tables[l][:].indirect(picked))
+            nc.vector.tensor_copy(values, tables[l][:].indirect(picked))
 
         def quantize(codes, scale_bytes, values):
             nc.vector.quantize_mx(out=codes.bitcast(FP8X4), scales=scale_bytes, in_=values.rearrange("p c t -> p (c t)"))
 
-        for l in range(PACK):
-            gather(l, 0, V)
-        gather(4, 0, V)
-        quantize(codes0[:], scales[0][:], grouped[0][:])
-        gather(5, 0, V)
-        gather(6, 0, V)
-        gather(7, 0, V - PLAIN)
-        for g in range(PASSES):
-            nc.scalar.copy(
-                w_grouped[g][:].rearrange("p (c i) t -> p c t i", i=PACK),
-                w_raw[g][:].rearrange("p t (c i) -> p c t i", i=PACK),
+        def interleave(copy, values, g, m0, m1):
+            copy(
+                values.rearrange("p (c i) t -> p c t i", i=PACK),
+                w_raw[g][:, :, m0:m1].rearrange("p t (c i) -> p c t i", i=PACK),
             )
-        last_plain = tail.tile([P, PLAIN], BF16, name="last_plain", align_bytes=256, offset=1024)
+
+        for l in range(PACK):
+            gather(grouped0[:, :, l], l, 0, V)
+        for t in range(PACK):
+            gather(grouped1[:, :, t], PACK + t, 0, HALF)
+            pair_halves = pairs[:, t // 2, :].bitcast(BF16).rearrange("p (v e) -> p v e", e=2)
+            gather(pair_halves[:, :, t % 2], PACK + t, HALF, V)
+            if t == 0:
+                quantize(codes0[:], scales[0][:], grouped0[:])
+
+        interleave(nc.scalar.copy, w_grouped0[:], 0, 0, N)
+        interleave(nc.scalar.copy, w_grouped1_scalar[:], 1, 0, N - SHARE)
+
         codes1_first = tail.tile([P, CHUNK], U32, name="codes1_first", align_bytes=256, offset=0)
-        codes1_rest = tail.tile([P, V - CHUNK], U32, name="codes1_rest", align_bytes=256, offset=2048)
+        w_grouped1_vector = tail.tile([P, SHARE, PACK], BF16, name="w_grouped1_vector", align_bytes=256, offset=512)
+        woven = tail.tile([P, HALF, PACK], BF16, name="woven", align_bytes=256, offset=1024)
+        for h in range(CHUNKS // 2):
+            points = slice(h * CHUNK, (h + 1) * CHUNK)
+            words = woven[:, points, :].rearrange("p v t -> p (v t)").bitcast(U32).rearrange("p (v u) -> p v u", u=2)
+            nc.scalar.copy(words, pairs[:, :, points].rearrange("p u v -> p v u"))
+
+        quantize(w_codes[0][:], w_scales[0][:], w_grouped0[:])
+        interleave(nc.vector.tensor_copy, w_grouped1_vector[:], 1, N - SHARE, N)
+        codes1_rest = tail.tile([P, V - CHUNK], U32, name="codes1_rest", align_bytes=256, offset=3072)
         codes = [
             [codes0[:, h * CHUNK : (h + 1) * CHUNK] for h in range(CHUNKS)],
             [codes1_first[:]] + [codes1_rest[:, h * CHUNK : (h + 1) * CHUNK] for h in range(CHUNKS - 1)],
         ]
+        chunk_values = [grouped1[:, :CHUNK, :], grouped1[:, CHUNK:, :], woven[:, :CHUNK, :], woven[:, CHUNK:, :]]
+
+        chunk_scales = [[scales[g][:, h * CHUNK : (h + 1) * CHUNK] for h in range(CHUNKS)] for g in range(PASSES)]
+        chunk_scales[1][1] = scales[0][4:, V - CHUNK :]
 
         def quantize_chunk(h):
-            points = slice(h * CHUNK, (h + 1) * CHUNK)
-            quantize(codes[1][h], scales[1][:, points], grouped[1][:, points, :])
+            quantize(codes[1][h], chunk_scales[1][h], chunk_values[h])
 
-        def multiply(g, h):
+        quantize_chunk(0)
+        quantize(w_codes[1][:, : N - SHARE], w_scales[1][:, : N - SHARE], w_grouped1_scalar[:])
+        quantize(w_codes[1][:, N - SHARE :], w_scales[1][:, N - SHARE :], w_grouped1_vector[:])
+        for h in range(1, CHUNKS):
+            quantize_chunk(h)
+
+        for g, h in ((0, 0), (0, 1), (0, 2), (1, 0), (1, 1), (0, 3), (1, 2), (1, 3)):
             nc.tensor.matmul_mx(
                 out=acc[h][:],
                 lhsT=w_codes[g][:].bitcast(FP8X4),
-                lhsT_scale=w_scales[g],
+                lhsT_scale=w_scales[g][:],
                 rhs=codes[g][h].bitcast(FP8X4),
-                rhs_scale=scales[g][:, h * CHUNK : (h + 1) * CHUNK],
+                rhs_scale=chunk_scales[g][h],
                 start=(g == 0),
                 stop=(g == PASSES - 1),
             )
-
-        quantize(w_codes[0][:], w_scales[0], w_grouped[0][:])
-        nc.vector.tensor_copy(last_plain[:], tables[7][:].indirect(offsets[:, LEVELS * COLS - PLAIN // 16 :]))
-        nc.scalar.copy(grouped[1][:, V - PLAIN :, PACK - 1], last_plain[:])
-        quantize_chunk(0)
-        quantize(w_codes[1][:], w_scales[1], w_grouped[1][:])
-        for h in range(1, CHUNKS):
-            quantize_chunk(h)
-        for g, h in ((0, 0), (0, 1), (0, 2), (1, 0), (1, 1), (1, 2), (0, 3), (1, 3)):
-            multiply(g, h)
         for h in range(CHUNKS):
             if h % 2 == 0:
                 nc.scalar.activation(result[h][:], acc[h][:], IDENTITY, bias=bias[:])

@@ -19,6 +19,7 @@ PACK = 4
 PASSES = K // (P * PACK)
 CHUNK = 128
 CHUNKS = V // CHUNK
+BLOCK = 32
 COLS = V // 16
 HALF = V // 2
 SHARE = N // 2
@@ -35,7 +36,9 @@ def tile_picked_grid_lin_bias_sub_l_kernel(tc, xT, w, b, offs, out):
         psum = ctx.enter_context(tc.psum_pool(name="psum", bufs=1))
 
         offsets = keep.tile([P, LEVELS * COLS], U16, name="offsets", align_bytes=256)
-        bias = keep.tile([P, 1], F32, name="bias")
+        bias_rows = keep.tile([P, BLOCK], F32, name="bias_rows", align_bytes=64)
+        bias_turned = keep.tile([P, BLOCK], F32, name="bias_turned", align_bytes=64)
+        bias = bias_turned[:, 0:1]
         tables = [keep.tile([P, T], F32, name=f"table{l}", align_bytes=256) for l in range(LEVELS)]
         w_raw = [tail.tile([P, PACK, N], F32, name=f"w_raw{g}", align_bytes=256, offset=3072 * g) for g in range(PASSES)]
         w_grouped0 = keep.tile([P, N, PACK], BF16, name="w_grouped0", align_bytes=64)
@@ -52,11 +55,13 @@ def tile_picked_grid_lin_bias_sub_l_kernel(tc, xT, w, b, offs, out):
 
         nc.sync.dma_start(tables[0][:], x_rows[0, 0])
         nc.sync.dma_start(offsets[:], offs)
+        nc.vector.memset(bias_rows[:], 0.0)
+        nc.sync.dma_start(bias_rows[0:P:BLOCK, :], b.rearrange("(q c) o -> q (c o)", c=BLOCK))
+        nc.vector.transpose(bias_turned[:], bias_rows[:])
         for l in range(1, LEVELS):
             nc.sync.dma_start(tables[l][:], x_rows[l // PACK, l % PACK])
         for g in range(PASSES):
             nc.sync.dma_start(w_raw[g][:], w_rows[g])
-        nc.sync.dma_start(bias[:], b)
 
         def gather(values, l, v0, v1):
             picked = offsets[:, l * COLS + v0 // 16 : l * COLS + v1 // 16]
@@ -124,7 +129,7 @@ def tile_picked_grid_lin_bias_sub_l_kernel(tc, xT, w, b, offs, out):
             )
         for h in range(CHUNKS):
             if h % 2 == 0:
-                nc.scalar.activation(result[h][:], acc[h][:], IDENTITY, bias=bias[:])
+                nc.scalar.activation(result[h][:], acc[h][:], IDENTITY, bias=bias)
             else:
-                nc.vector.tensor_scalar(result[h][:], acc[h][:], bias[:], None, ADD)
+                nc.vector.tensor_scalar(result[h][:], acc[h][:], bias, None, ADD)
             nc.sync.dma_start(out[:, h * CHUNK : (h + 1) * CHUNK], result[h][:])

@@ -19,6 +19,7 @@ PACK = 4
 PASSES = K // (P * PACK)
 CHUNK = 128
 CHUNKS = V // CHUNK
+LOADS = ((0, 2), (2, 1), (3, 1), (4, 1), (5, 1), (6, 1), (7, 1))
 BLOCK = 32
 COLS = V // 16
 HALF = V // 2
@@ -27,7 +28,7 @@ SHARE = N // 2
 
 def tile_picked_grid_lin_bias_sub_l_kernel(tc, xT, w, b, offs, out):
     nc = tc.nc
-    x_rows = xT.rearrange("(g p t) c -> g t p c", p=P, t=PACK)
+    x_rows = xT.rearrange("(g p t) c -> g p (t c)", p=P, t=PACK)
     w_rows = w.rearrange("(g p t) m -> g p t m", p=P, t=PACK)
 
     with ExitStack() as ctx:
@@ -39,7 +40,8 @@ def tile_picked_grid_lin_bias_sub_l_kernel(tc, xT, w, b, offs, out):
         bias_rows = keep.tile([P, BLOCK], F32, name="bias_rows", align_bytes=64)
         bias_turned = keep.tile([P, BLOCK], F32, name="bias_turned", align_bytes=64)
         bias = bias_turned[:, 0:1]
-        tables = [keep.tile([P, T], F32, name=f"table{l}", align_bytes=256) for l in range(LEVELS)]
+        loads = [keep.tile([P, count * T], F32, name=f"load{first}", align_bytes=256) for first, count in LOADS]
+        tables = [tile[:, i * T : (i + 1) * T] for tile, (first, count) in zip(loads, LOADS) for i in range(count)]
         w_raw = [tail.tile([P, PACK, N], F32, name=f"w_raw{g}", align_bytes=256, offset=3072 * g) for g in range(PASSES)]
         w_grouped0 = keep.tile([P, N, PACK], BF16, name="w_grouped0", align_bytes=64)
         w_grouped1_scalar = keep.tile([P, N - SHARE, PACK], BF16, name="w_grouped1_scalar", align_bytes=64)
@@ -53,19 +55,23 @@ def tile_picked_grid_lin_bias_sub_l_kernel(tc, xT, w, b, offs, out):
         acc = [psum.tile([N, CHUNK], F32, name=f"acc{h}") for h in range(CHUNKS)]
         result = [keep.tile([N, CHUNK], F32, name=f"result{h}", align_bytes=256) for h in range(CHUNKS)]
 
-        nc.sync.dma_start(tables[0][:], x_rows[0, 0])
-        nc.sync.dma_start(offsets[:], offs)
-        nc.vector.memset(bias_rows[:], 0.0)
-        nc.sync.dma_start(bias_rows[0:P:BLOCK, :], b.rearrange("(q c) o -> q (c o)", c=BLOCK))
-        nc.vector.transpose(bias_turned[:], bias_rows[:])
-        for l in range(1, LEVELS):
-            nc.sync.dma_start(tables[l][:], x_rows[l // PACK, l % PACK])
+        def load_small():
+            nc.sync.dma_start(offsets[:], offs)
+            nc.vector.memset(bias_rows[:], 0.0)
+            nc.sync.dma_start(bias_rows[0:P:BLOCK, :], b.rearrange("(q c) o -> q (c o)", c=BLOCK))
+            nc.vector.transpose(bias_turned[:], bias_rows[:])
+
+        for tile, (first, count) in zip(loads, LOADS):
+            t = first % PACK
+            nc.sync.dma_start(tile[:], x_rows[first // PACK][:, t * T : (t + count) * T])
+            if first == 0:
+                load_small()
         for g in range(PASSES):
             nc.sync.dma_start(w_raw[g][:], w_rows[g])
 
         def gather(values, l, v0, v1):
             picked = offsets[:, l * COLS + v0 // 16 : l * COLS + v1 // 16]
-            nc.vector.tensor_copy(values, tables[l][:].indirect(picked))
+            nc.vector.tensor_copy(values, tables[l].indirect(picked))
 
         def quantize(codes, scale_bytes, values):
             nc.vector.quantize_mx(out=codes.bitcast(FP8X4), scales=scale_bytes, in_=values.rearrange("p c t -> p (c t)"))

@@ -112,7 +112,7 @@ def tile_picked_grid_lin_bias_sub_l_kernel(tc, xT, w, b, offs, out):
         chunk_values = [grouped1[:, :CHUNK, :], grouped1[:, CHUNK:, :], woven[:, :CHUNK, :], woven[:, CHUNK:, :]]
 
         chunk_scales = [[scales[g][:, h * CHUNK : (h + 1) * CHUNK] for h in range(CHUNKS)] for g in range(PASSES)]
-        chunk_scales[1][1] = scales[0][4:, V - CHUNK :]
+        chunk_scales[1][2] = scales[0][4:, V - CHUNK :]
 
         def quantize_chunk(h):
             quantize(codes[1][h], chunk_scales[1][h], chunk_values[h])
@@ -123,7 +123,7 @@ def tile_picked_grid_lin_bias_sub_l_kernel(tc, xT, w, b, offs, out):
         for h in range(1, CHUNKS):
             quantize_chunk(h)
 
-        for g, h in ((0, 0), (0, 1), (0, 2), (1, 0), (1, 1), (0, 3), (1, 2), (1, 3)):
+        for g, h in ((0, 0), (0, 1), (0, 2), (1, 0), (1, 1), (1, 2), (0, 3), (1, 3)):
             nc.tensor.matmul_mx(
                 out=acc[h][:],
                 lhsT=w_codes[g][:].bitcast(FP8X4),

@@ -19,7 +19,7 @@ PACK = 4
 PASSES = K // (P * PACK)
 CHUNK = 128
 CHUNKS = V // CHUNK
-LOADS = ((0, 2), (2, 1), (3, 1), (4, 1), (5, 1), (6, 1), (7, 1))
+LOADS = ((0, 2), (2, 2), (4, 2), (6, 1), (7, 1))
 BLOCK = 32
 COLS = V // 16
 HALF = V // 2
@@ -49,7 +49,7 @@ def tile_picked_grid_lin_bias_sub_l_kernel(tc, xT, w, b, offs, out):
         w_scales = [keep.tile([P, N], U8, name=f"w_scales{g}", align_bytes=64) for g in range(PASSES)]
         grouped0 = keep.tile([P, V, PACK], BF16, name="grouped0", align_bytes=64)
         grouped1 = keep.tile([P, HALF, PACK], BF16, name="grouped1", align_bytes=64)
-        pairs = keep.tile([P, 2, HALF], U32, name="pairs", align_bytes=64)
+        pairs = keep.tile([P, 3, HALF], U32, name="pairs", align_bytes=64)
         codes0 = keep.tile([P, V], U32, name="codes0", align_bytes=64)
         scales = [keep.tile([P, V], U8, name=f"scales{g}", align_bytes=64) for g in range(PASSES)]
         acc = [psum.tile([N, CHUNK], F32, name=f"acc{h}") for h in range(CHUNKS)]
@@ -58,7 +58,9 @@ def tile_picked_grid_lin_bias_sub_l_kernel(tc, xT, w, b, offs, out):
         def load_small():
             nc.sync.dma_start(offsets[:], offs)
             nc.vector.memset(bias_rows[:], 0.0)
-            nc.sync.dma_start(bias_rows[0:P:BLOCK, :], b.rearrange("(q c) o -> q (c o)", c=BLOCK))
+            b_rows = b.rearrange("(q c) o -> q (c o)", c=BLOCK)
+            for c0, c1 in ((0, 16), (16, 24), (24, 32)):
+                nc.sync.dma_start(bias_rows[0:P:BLOCK, c0:c1], b_rows[:, c0:c1])
             nc.vector.transpose(bias_turned[:], bias_rows[:])
 
         for tile, (first, count) in zip(loads, LOADS):
@@ -84,12 +86,18 @@ def tile_picked_grid_lin_bias_sub_l_kernel(tc, xT, w, b, offs, out):
 
         for l in range(PACK):
             gather(grouped0[:, :, l], l, 0, V)
-        for t in range(PACK):
+        quantize(codes0[:], scales[0][:], grouped0[:])
+
+        def halves(words):
+            return words.bitcast(BF16).rearrange("p (v e) -> p v e", e=2)
+
+        for t in range(2):
+            gather(halves(pairs[:, 0:2, :].rearrange("p u v -> p (u v)"))[:, :, t], PACK + t, 0, V)
+        grouped1_words = grouped1[:].rearrange("p v t -> p (v t)").bitcast(U32).rearrange("p (v u) -> p v u", u=2)
+        nc.scalar.copy(grouped1_words[:, :, 0], pairs[:, 0, :])
+        for t in range(2, PACK):
             gather(grouped1[:, :, t], PACK + t, 0, HALF)
-            pair_halves = pairs[:, t // 2, :].bitcast(BF16).rearrange("p (v e) -> p v e", e=2)
-            gather(pair_halves[:, :, t % 2], PACK + t, HALF, V)
-            if t == 0:
-                quantize(codes0[:], scales[0][:], grouped0[:])
+            gather(halves(pairs[:, 2, :])[:, :, t % 2], PACK + t, HALF, V)
 
         interleave(nc.scalar.copy, w_grouped0[:], 0, 0, N)
         interleave(nc.scalar.copy, w_grouped1_scalar[:], 1, 0, N - SHARE)
@@ -100,7 +108,7 @@ def tile_picked_grid_lin_bias_sub_l_kernel(tc, xT, w, b, offs, out):
         for h in range(CHUNKS // 2):
             points = slice(h * CHUNK, (h + 1) * CHUNK)
             words = woven[:, points, :].rearrange("p v t -> p (v t)").bitcast(U32).rearrange("p (v u) -> p v u", u=2)
-            nc.scalar.copy(words, pairs[:, :, points].rearrange("p u v -> p v u"))
+            nc.scalar.copy(words, pairs[:, 1:, points].rearrange("p u v -> p v u"))
 
         quantize(w_codes[0][:], w_scales[0][:], w_grouped0[:])
         interleave(nc.vector.tensor_copy, w_grouped1_vector[:], 1, N - SHARE, N)

@@ -20,6 +20,7 @@ PASSES = K // (P * PACK)
 CHUNK = 128
 CHUNKS = V // CHUNK
 LOADS = ((0, 2), (2, 2), (4, 2), (6, 1), (7, 1))
+BIAS_LOADS = 4
 BLOCK = 32
 COLS = V // 16
 HALF = V // 2
@@ -59,8 +60,9 @@ def tile_picked_grid_lin_bias_sub_l_kernel(tc, xT, w, b, offs, out):
             nc.sync.dma_start(offsets[:], offs)
             nc.vector.memset(bias_rows[:], 0.0)
             b_rows = b.rearrange("(q c) o -> q (c o)", c=BLOCK)
-            for c0, c1 in ((0, 16), (16, 24), (24, 32)):
-                nc.sync.dma_start(bias_rows[0:P:BLOCK, c0:c1], b_rows[:, c0:c1])
+            for c in range(0, BLOCK, BLOCK // BIAS_LOADS):
+                columns = slice(c, c + BLOCK // BIAS_LOADS)
+                nc.sync.dma_start(bias_rows[0:P:BLOCK, columns], b_rows[:, columns])
             nc.vector.transpose(bias_turned[:], bias_rows[:])
 
         for tile, (first, count) in zip(loads, LOADS):

from contextlib import ExitStack

import concourse.mybir as mybir

K, T, LEVELS, V, N = 1024, 2048, 8, 512, 128
FLOPS = 2 * K * N * V

F32 = mybir.dt.float32
BF16 = mybir.dt.bfloat16
U32 = mybir.dt.uint32
U16 = mybir.dt.uint16
U8 = mybir.dt.uint8
FP8X4 = mybir.dt.float8_e4m3fn_x4
ADD = mybir.AluOpType.add
IDENTITY = mybir.ActivationFunctionType.Identity

P = 128
PACK = 4
PASSES = K // (P * PACK)
CHUNK = 128
CHUNKS = V // CHUNK
LOADS = ((0, 2), (2, 2), (4, 2), (6, 1), (7, 1))
BIAS_LOADS = 4
BLOCK = 32
COLS = V // 16
HALF = V // 2
SHARE = N // 2


def tile_picked_grid_lin_bias_sub_l_kernel(tc, xT, w, b, offs, out):
    nc = tc.nc
    x_rows = xT.rearrange("(g p t) c -> g p (t c)", p=P, t=PACK)
    w_rows = w.rearrange("(g p t) m -> g p t m", p=P, t=PACK)

    with ExitStack() as ctx:
        keep = ctx.enter_context(tc.tile_pool(name="keep", bufs=1))
        tail = ctx.enter_context(tc.tile_pool(name="tail", bufs=1))
        psum = ctx.enter_context(tc.psum_pool(name="psum", bufs=1))

        offsets = keep.tile([P, LEVELS * COLS], U16, name="offsets", align_bytes=256)
        bias_rows = keep.tile([P, BLOCK], F32, name="bias_rows", align_bytes=64)
        bias_turned = keep.tile([P, BLOCK], F32, name="bias_turned", align_bytes=64)
        bias = bias_turned[:, 0:1]
        loads = [keep.tile([P, count * T], F32, name=f"load{first}", align_bytes=256) for first, count in LOADS]
        tables = [tile[:, i * T : (i + 1) * T] for tile, (first, count) in zip(loads, LOADS) for i in range(count)]
        w_raw = [tail.tile([P, PACK, N], F32, name=f"w_raw{g}", align_bytes=256, offset=3072 * g) for g in range(PASSES)]
        w_grouped0 = keep.tile([P, N, PACK], BF16, name="w_grouped0", align_bytes=64)
        w_grouped1_scalar = keep.tile([P, N - SHARE, PACK], BF16, name="w_grouped1_scalar", align_bytes=64)
        w_codes = [keep.tile([P, N], U32, name=f"w_codes{g}", align_bytes=64) for g in range(PASSES)]
        w_scales = [keep.tile([P, N], U8, name=f"w_scales{g}", align_bytes=64) for g in range(PASSES)]
        grouped0 = keep.tile([P, V, PACK], BF16, name="grouped0", align_bytes=64)
        grouped1 = keep.tile([P, HALF, PACK], BF16, name="grouped1", align_bytes=64)
        pairs = keep.tile([P, 3, HALF], U32, name="pairs", align_bytes=64)
        codes0 = keep.tile([P, V], U32, name="codes0", align_bytes=64)
        scales = [keep.tile([P, V], U8, name=f"scales{g}", align_bytes=64) for g in range(PASSES)]
        acc = [psum.tile([N, CHUNK], F32, name=f"acc{h}") for h in range(CHUNKS)]
        result = [keep.tile([N, CHUNK], F32, name=f"result{h}", align_bytes=256) for h in range(CHUNKS)]

        def load_small():
            nc.sync.dma_start(offsets[:], offs)
            nc.vector.memset(bias_rows[:], 0.0)
            b_rows = b.rearrange("(q c) o -> q (c o)", c=BLOCK)
            for c in range(0, BLOCK, BLOCK // BIAS_LOADS):
                columns = slice(c, c + BLOCK // BIAS_LOADS)
                nc.sync.dma_start(bias_rows[0:P:BLOCK, columns], b_rows[:, columns])
            nc.vector.transpose(bias_turned[:], bias_rows[:])

        for tile, (first, count) in zip(loads, LOADS):
            t = first % PACK
            nc.sync.dma_start(tile[:], x_rows[first // PACK][:, t * T : (t + count) * T])
            if first == 0:
                load_small()
        for g in range(PASSES):
            nc.sync.dma_start(w_raw[g][:], w_rows[g])

        def gather(values, l, v0, v1):
            picked = offsets[:, l * COLS + v0 // 16 : l * COLS + v1 // 16]
            nc.vector.tensor_copy(values, tables[l].indirect(picked))

        def quantize(codes, scale_bytes, values):
            nc.vector.quantize_mx(out=codes.bitcast(FP8X4), scales=scale_bytes, in_=values.rearrange("p c t -> p (c t)"))

        def interleave(copy, values, g, m0, m1):
            copy(
                values.rearrange("p (c i) t -> p c t i", i=PACK),
                w_raw[g][:, :, m0:m1].rearrange("p t (c i) -> p c t i", i=PACK),
            )

        for l in range(PACK):
            gather(grouped0[:, :, l], l, 0, V)
        quantize(codes0[:], scales[0][:], grouped0[:])

        def halves(words):
            return words.bitcast(BF16).rearrange("p (v e) -> p v e", e=2)

        for t in range(2):
            gather(halves(pairs[:, 0:2, :].rearrange("p u v -> p (u v)"))[:, :, t], PACK + t, 0, V)
        grouped1_words = grouped1[:].rearrange("p v t -> p (v t)").bitcast(U32).rearrange("p (v u) -> p v u", u=2)
        nc.scalar.copy(grouped1_words[:, :, 0], pairs[:, 0, :])
        for t in range(2, PACK):
            gather(grouped1[:, :, t], PACK + t, 0, HALF)
            gather(halves(pairs[:, 2, :])[:, :, t % 2], PACK + t, HALF, V)

        interleave(nc.scalar.copy, w_grouped0[:], 0, 0, N)
        interleave(nc.scalar.copy, w_grouped1_scalar[:], 1, 0, N - SHARE)

        codes1_first = tail.tile([P, CHUNK], U32, name="codes1_first", align_bytes=256, offset=0)
        w_grouped1_vector = tail.tile([P, SHARE, PACK], BF16, name="w_grouped1_vector", align_bytes=256, offset=512)
        woven = tail.tile([P, HALF, PACK], BF16, name="woven", align_bytes=256, offset=1024)
        for h in range(CHUNKS // 2):
            points = slice(h * CHUNK, (h + 1) * CHUNK)
            words = woven[:, points, :].rearrange("p v t -> p (v t)").bitcast(U32).rearrange("p (v u) -> p v u", u=2)
            nc.scalar.copy(words, pairs[:, 1:, points].rearrange("p u v -> p v u"))

        quantize(w_codes[0][:], w_scales[0][:], w_grouped0[:])
        interleave(nc.vector.tensor_copy, w_grouped1_vector[:], 1, N - SHARE, N)
        codes1_rest = tail.tile([P, V - CHUNK], U32, name="codes1_rest", align_bytes=256, offset=3072)
        codes = [
            [codes0[:, h * CHUNK : (h + 1) * CHUNK] for h in range(CHUNKS)],
            [codes1_first[:]] + [codes1_rest[:, h * CHUNK : (h + 1) * CHUNK] for h in range(CHUNKS - 1)],
        ]
        chunk_values = [grouped1[:, :CHUNK, :], grouped1[:, CHUNK:, :], woven[:, :CHUNK, :], woven[:, CHUNK:, :]]

        chunk_scales = [[scales[g][:, h * CHUNK : (h + 1) * CHUNK] for h in range(CHUNKS)] for g in range(PASSES)]
        chunk_scales[1][2] = scales[0][4:, V - CHUNK :]

        def quantize_chunk(h):
            quantize(codes[1][h], chunk_scales[1][h], chunk_values[h])

        quantize_chunk(0)
        quantize(w_codes[1][:, : N - SHARE], w_scales[1][:, : N - SHARE], w_grouped1_scalar[:])
        quantize(w_codes[1][:, N - SHARE :], w_scales[1][:, N - SHARE :], w_grouped1_vector[:])
        for h in range(1, CHUNKS):
            quantize_chunk(h)

        for g, h in ((0, 0), (0, 1), (0, 2), (1, 0), (1, 1), (1, 2), (0, 3), (1, 3)):
            nc.tensor.matmul_mx(
                out=acc[h][:],
                lhsT=w_codes[g][:].bitcast(FP8X4),
                lhsT_scale=w_scales[g][:],
                rhs=codes[g][h].bitcast(FP8X4),
                rhs_scale=chunk_scales[g][h],
                start=(g == 0),
                stop=(g == PASSES - 1),
            )
        for h in range(CHUNKS):
            if h % 2 == 0:
                nc.scalar.activation(result[h][:], acc[h][:], IDENTITY, bias=bias)
            else:
                nc.vector.tensor_scalar(result[h][:], acc[h][:], bias, None, ADD)
            nc.sync.dma_start(out[:, h * CHUNK : (h + 1) * CHUNK], result[h][:])
